import numpy as np
import ml_dtypes


def mxq(x, axis, fmt="e4m3"):
    dtype, down = {"e4m3": (ml_dtypes.float8_e4m3fn, 7), "e5m2": (ml_dtypes.float8_e5m2, 14)}[fmt]
    v = np.moveaxis(np.asarray(x, np.float32).astype(ml_dtypes.bfloat16).astype(np.float64), axis, -1)
    blocks = v.reshape(v.shape[:-1] + (-1, 32))
    amax = np.abs(blocks).max(-1, keepdims=True)
    byte = np.maximum(np.where(amax > 0, np.frexp(amax)[1] - 1 + 127, 0) - down, 1)
    scale = np.exp2(byte - 127.0)
    codes = (blocks / scale).astype(np.float32).astype(dtype).astype(np.float64)
    return np.moveaxis((codes * scale).reshape(v.shape), -1, axis)


WIDE = False


def mx_kscale(k):
    if not WIDE:
        return np.ones(k)
    levels = np.array([10, -10, 5, -5, 0])
    if k % 512:
        return np.exp2(np.random.permutation(np.resize(levels, k // 32))).repeat(32)
    a = np.empty((k // 512, 16))
    for p in range(k // 512):
        a[p, :8] = np.random.permutation(np.resize(levels, 8))
        for g in range(8):
            far = levels[np.abs(levels - a[p, g]) >= 10]
            a[p, g + 8] = far[np.random.randint(len(far))]
    return np.exp2(a.ravel()).repeat(32)


def f64(x):
    return np.asarray(x).astype(np.float64)


def striped(idx):
    return np.tile(idx.reshape(-1, 16).T, (8, 1)).astype(np.uint16)


def unstriped(offs):
    return offs[:16].T.reshape(-1).astype(np.int64)


E2M1 = np.array([0.0, 0.5, 1.0, 1.5, 2.0, 3.0, 4.0, 6.0, -0.0, -0.5, -1.0, -1.5, -2.0, -3.0, -4.0, -6.0])


def pack_weight(w, fmt):
    k, n = w.shape
    w = f64(np.asarray(w, np.float32).astype(ml_dtypes.bfloat16)).reshape(k // 32, 32, n)
    amax = np.abs(w).max(1)
    if fmt == "e4m3":
        byte = np.frexp(amax)[1] - 1 + 127 - 7
    else:
        mant, ex = np.frexp(amax / 6.0)
        byte = np.where(mant > 0.5, ex, ex - 1) + 127
    byte = np.clip(np.where(amax > 0, byte, 1), 1, 254)
    scaled = (w * np.exp2(127.0 - byte)[:, None, :]).reshape(k, n).astype(np.float32)
    by_word = np.ascontiguousarray(scaled.reshape(k // 512, 128, 4, n).transpose(0, 1, 3, 2))
    if fmt == "e4m3":
        words = by_word.astype(ml_dtypes.float8_e4m3fn).view(np.uint8)
    else:
        c = by_word.astype(ml_dtypes.float4_e2m1fn).view(np.uint8) & 0xF
        words = (c[..., 0::2] | (c[..., 1::2] << 4)).reshape(k // 512, 128, 2 * n)
    return np.ascontiguousarray(words), np.ascontiguousarray(byte.astype(np.uint8).reshape(k // 512, 16, n))


def unpack_weight(words, scales, fmt):
    g, _, n = scales.shape
    words = np.ascontiguousarray(words).reshape(g, 128, n, -1)
    if fmt == "e4m3":
        vals = words.view(ml_dtypes.float8_e4m3fn).astype(np.float64)
    else:
        nib = np.empty((g, 128, n, 4), np.uint8)
        nib[..., 0::2] = words & 0xF
        nib[..., 1::2] = words >> 4
        vals = E2M1[nib]
    vals = vals * np.repeat(np.exp2(scales.astype(np.float64) - 127.0), 8, axis=1)[..., None]
    return vals.transpose(0, 1, 3, 2).reshape(g * 512, n)


def gelu(v):
    return 0.5 * v * (1.0 + np.tanh(np.sqrt(2.0 / np.pi) * (v + 0.044715 * v**3)))


def twice(P):
    return np.random.permutation(np.repeat(np.arange(P), 2))


K, T, S, P, H = 512, 4096, 1024, 512, 1024

def setup_inputs():
    n = np.random.standard_normal
    s = mx_kscale(K)[:, None]
    u = mx_kscale(H)[:, None]
    d = {}
    d["tab_words"], d["tab_scales"] = pack_weight(n((K, T)) * s, "e4m3")
    d["offs"] = striped(np.random.permutation(T)[:S])
    d["pos1"] = striped(np.random.permutation(S)[:P])
    d["pos2"] = striped(np.random.permutation(S)[:P])
    d["pos3"] = striped(twice(P))
    d["w1"] = (n((K, H)) / K**0.5 / s * u.T).astype(np.float32)
    d["w2"] = (n((K, H)) / K**0.5 / s * u.T).astype(np.float32)
    d["w3_words"], d["w3_scales"] = pack_weight(n((K, H)) / K**0.5 / s * u.T, "e2m1")
    d["w4_words"], d["w4_scales"] = pack_weight(0.7 * n((H, H)) / H**0.5 / u, "e4m3")
    d["gh"] = (np.exp(0.3 * n(H)) / u[:, 0]).astype(np.float32)
    return d

def reference(tab_words, tab_scales, offs, pos1, pos2, pos3, w1, w2, w3_words, w3_scales, w4_words, w4_scales, gh):
    v = unpack_weight(tab_words, tab_scales, "e4m3")[:, unstriped(offs)]
    stain = mxq(f64(w1), 0, "e4m3").T @ v
    crease = mxq(f64(w2), 0, "e4m3").T @ v
    clean = unpack_weight(w3_words, w3_scales, "e2m1").T @ v
    h = np.maximum(stain, crease) - clean
    z = h[:, unstriped(pos1)] + h[:, unstriped(pos2)]
    y = unpack_weight(w4_words, w4_scales, "e4m3").T @ mxq(z, 0, "e4m3")
    yup = y[:, unstriped(pos3)]
    hs = f64(gh)[:, None] * h
    return np.sqrt(np.square(yup) + np.square(hs))

@@ -1,0 +1,328 @@
+from contextlib import ExitStack
+
+import concourse.mybir as mybir
+
+K, T, S, NOTES, H = 512, 4096, 1024, 512, 1024
+FLOPS = 3 * 2 * K * H * S + 2 * H * H * NOTES
+
+F32 = mybir.dt.float32
+BF16 = mybir.dt.bfloat16
+I32 = mybir.dt.int32
+U32 = mybir.dt.uint32
+U16 = mybir.dt.uint16
+U8 = mybir.dt.uint8
+FP8X4 = mybir.dt.float8_e4m3fn_x4
+FP4X4 = mybir.dt.float4_e2m1fn_x4
+ALU = mybir.AluOpType
+ACT = mybir.ActivationFunctionType
+
+P = 128
+PACK = 4
+PASS = P * PACK
+BANK = 512
+TILES = H // P
+LIST = 16
+
+
+def tile_list_note_soiling_grade_kernel(
+    tc, tab_words, tab_scales, offs, pos1, pos2, pos3, w1, w2, w3_words, w3_scales, w4_words, w4_scales, gh, out
+):
+    nc = tc.nc
+    with ExitStack() as ctx:
+        keep = ctx.enter_context(tc.tile_pool(name="keep", bufs=1))
+        ring2 = ctx.enter_context(tc.tile_pool(name="ring2", bufs=2))
+        ring3 = ctx.enter_context(tc.tile_pool(name="ring3", bufs=3))
+        psum = ctx.enter_context(tc.psum_pool(name="psum", bufs=2))
+
+        offs_sb = keep.tile([P, S // LIST], U16, name="offs_sb")
+        pos1_sb = keep.tile([P, NOTES // LIST], U16, name="pos1_sb")
+        pos2_sb = keep.tile([P, NOTES // LIST], U16, name="pos2_sb")
+        pos3_sb = keep.tile([P, S // LIST], U16, name="pos3_sb")
+
+        tabw = keep.tile([P, T], I32, name="tabw", align_bytes=64)
+        tabs = keep.tile([P, T], U8, name="tabs", align_bytes=64)
+        w3w_raw = keep.tile([P, 2 * H], U8, name="w3w_raw", align_bytes=64)
+        w3s_raw = keep.tile([P, H], U8, name="w3s_raw", align_bytes=64)
+        w4s_raw = keep.tile([P, H], U8, name="w4s_raw", align_bytes=64)
+        w4w_raw = [keep.tile([P, H], I32, name="w4w_raw%d" % a, align_bytes=64) for a in range(2)]
+        gh_sb = keep.tile([P, 2, PACK], F32, name="gh_sb")
+        raw = {}
+        for wi in range(2):
+            for b in range(2):
+                for mh in range(2):
+                    raw[wi, b, mh] = keep.tile([P, PACK, 256], F32, name="raw%d%d%d" % (wi, b, mh), align_bytes=64)
+
+        nc.vector.memset(tabs[:].bitcast(I32), 0)
+        nc.gpsimd.memset(w3s_raw[:].bitcast(I32), 0)
+        nc.gpsimd.memset(w4s_raw[:].bitcast(I32), 0)
+
+        def load_raw(wi, b, mh):
+            w = (w1, w2)[wi]
+            c0 = PASS * b + 256 * mh
+            nc.sync.dma_start(raw[wi, b, mh][:], w[:, c0 : c0 + 256].rearrange("(p j) c -> p j c", j=PACK))
+
+        nc.sync.dma_start(offs_sb[:], offs)
+        load_raw(0, 0, 0)
+        for q in range(4):
+            nc.sync.dma_start(tabs[32 * q : 32 * q + 4, :].bitcast(I32), tab_scales[0, 4 * q : 4 * q + 4, :].bitcast(I32))
+        load_raw(0, 0, 1)
+        nc.sync.dma_start(tabw[:], tab_words[0].rearrange("p t i -> p (t i)").bitcast(I32))
+        for q in range(4):
+            nc.sync.dma_start(w3s_raw[32 * q : 32 * q + 4, :].bitcast(I32), w3_scales[0, 4 * q : 4 * q + 4, :].bitcast(I32))
+        nc.sync.dma_start(w3w_raw[:].bitcast(I32), w3_words[0].bitcast(I32))
+        load_raw(1, 0, 0)
+        load_raw(1, 0, 1)
+        nc.sync.dma_start(pos1_sb[:], pos1)
+        nc.sync.dma_start(pos2_sb[:], pos2)
+        nc.sync.dma_start(gh_sb[:], gh.rearrange("(b p t) -> p b t", b=2, t=PACK))
+        for wi in range(2):
+            for mh in range(2):
+                load_raw(wi, 1, mh)
+        for a in range(2):
+            nc.sync.dma_start(w4w_raw[a][:], w4_words[a].rearrange("p c i -> p (c i)").bitcast(I32))
+        for q in range(4):
+            nc.sync.dma_start(w4s_raw[32 * q : 32 * q + 8, :].bitcast(I32), w4_scales[:, 4 * q : 4 * q + 4, :].bitcast(I32))
+        nc.sync.dma_start(pos3_sb[:], pos3)
+
+        vw = [keep.tile([P, BANK], U32, name="vw%d" % jh, align_bytes=64) for jh in range(2)]
+        vs = [keep.tile([P, BANK], U8, name="vs%d" % jh, align_bytes=64) for jh in range(2)]
+        cols = BANK // LIST
+        for jh in range(2):
+            nc.vector.tensor_copy(vs[jh][:], tabs[:].indirect(offs_sb[:, jh * cols : (jh + 1) * cols]))
+
+        grouped = {}
+        wq = {}
+        ws = {}
+
+        def cast(wi, b, mh, eng):
+            if (wi, b) not in grouped:
+                grouped[wi, b] = ring2.tile([P, PACK, P, PACK], BF16, name="grouped", align_bytes=64)
+            dst = grouped[wi, b][:, :, 64 * mh : 64 * (mh + 1), :].rearrange("p t m j -> p m j t")
+            src = raw[wi, b, mh][:].rearrange("p j (m t) -> p m j t", t=PACK)
+            if eng == "act":
+                nc.scalar.copy(dst, src)
+            else:
+                nc.vector.tensor_copy(dst, src)
+
+        def quant(wi, b):
+            wq[wi, b] = keep.tile([P, PASS], U32, name="wq%d%d" % (wi, b), align_bytes=64)
+            ws[wi, b] = keep.tile([P, PASS], U8, name="ws%d%d" % (wi, b), align_bytes=64)
+            nc.vector.quantize_mx(
+                out=wq[wi, b][:].bitcast(FP8X4),
+                scales=ws[wi, b][:],
+                in_=grouped[wi, b][:].rearrange("p t m j -> p (t m j)"),
+            )
+
+        w3w = [keep.tile([P, 2 * PASS], U8, name="w3w%d" % b, align_bytes=64) for b in range(2)]
+        w3s = [keep.tile([P, PASS], U8, name="w3s%d" % b, align_bytes=64) for b in range(2)]
+
+        def deal_w3(b):
+            nc.vector.tensor_copy(
+                w3w[b][:].bitcast(U16).rearrange("p (t m) -> p m t", t=PACK),
+                w3w_raw[:, 2 * PASS * b : 2 * PASS * (b + 1)].bitcast(U16).rearrange("p (m t) -> p m t", t=PACK),
+            )
+            nc.gpsimd.tensor_copy(
+                w3s[b][:].rearrange("p (t m) -> p t m", t=PACK),
+                w3s_raw[:, PASS * b : PASS * (b + 1)].rearrange("p (m t) -> p t m", t=PACK),
+            )
+
+        cast(0, 0, 0, "act")
+        cast(0, 0, 1, "act")
+        quant(0, 0)
+        for jh in range(2):
+            nc.vector.tensor_copy(vw[jh][:], tabw[:].bitcast(U32).indirect(offs_sb[:, jh * cols : (jh + 1) * cols]))
+        cast(1, 0, 0, "act")
+        cast(1, 0, 1, "dve")
+        quant(1, 0)
+        deal_w3(0)
+
+        w4w = [keep.tile([P, H], U32, name="w4w%d" % a, align_bytes=64) for a in range(2)]
+        w4s = keep.tile([P, H], U8, name="w4s", align_bytes=64)
+
+        def deal_w4(a):
+            for b in range(2):
+                nc.scalar.copy(
+                    w4w[a][:, PASS * b : PASS * (b + 1)].rearrange("p (t m) -> p m t", t=PACK),
+                    w4w_raw[a][:, PASS * b : PASS * (b + 1)].bitcast(U32).rearrange("p (m t) -> p m t", t=PACK),
+                )
+
+        def deal_w4s():
+            nc.gpsimd.tensor_copy(
+                w4s[:].rearrange("p (b t m) -> p b t m", b=2, t=PACK),
+                w4s_raw[:].rearrange("p (b m t) -> p b t m", b=2, t=PACK),
+            )
+
+        hsq = [keep.tile([P, S], F32, name="hsq%d" % i) for i in range(TILES)]
+        zsum = [keep.tile([P, PACK, NOTES], F32, name="zsum%d" % b) for b in range(2)]
+        zb = [keep.tile([P, NOTES, PACK], BF16, name="zb%d" % b, align_bytes=64) for b in range(2)]
+        zq = [keep.tile([P, NOTES], U32, name="zq%d" % b, align_bytes=64) for b in range(2)]
+        zs = [keep.tile([P, NOTES], U8, name="zs%d" % b, align_bytes=64) for b in range(2)]
+        h = {}
+        banks = {}
+        worse = {}
+        front = {}
+
+        def products(i, jh):
+            b, t = divmod(i, PACK)
+            c = slice(P * t, P * (t + 1))
+            pa = psum.tile([P, BANK], F32, name="pa")
+            pb = psum.tile([P, BANK], F32, name="pb")
+            pc = psum.tile([P, BANK], F32, name="pc")
+            rhs = vw[jh][:].bitcast(FP8X4)
+            for acc, wi in ((pa, 0), (pb, 1)):
+                nc.tensor.matmul_mx(
+                    out=acc[:], lhsT=wq[wi, b][:, c].bitcast(FP8X4), lhsT_scale=ws[wi, b][:, c],
+                    rhs=rhs, rhs_scale=vs[jh][:], start=True, stop=True,
+                )
+            nc.tensor.matmul_mx(
+                out=pc[:], lhsT=w3w[b][:, 2 * P * t : 2 * P * (t + 1)].bitcast(FP4X4), lhsT_scale=w3s[b][:, c],
+                rhs=rhs, rhs_scale=vs[jh][:], start=True, stop=True,
+            )
+            stain = ring3.tile([P, BANK], F32, name="stain")
+            nc.scalar.copy(stain[:], pa[:])
+            banks[i, jh] = (stain, pb, pc)
+
+        def take_max(i, jh):
+            stain, pb, pc = banks[i, jh]
+            worse[i, jh] = ring3.tile([P, BANK], F32, name="worse")
+            nc.vector.tensor_tensor(worse[i, jh][:], pb[:], stain[:], ALU.max)
+
+        def take_diff(i, jh):
+            if jh == 0:
+                h[i] = ring3.tile([P, S], F32, name="h")
+            nc.vector.tensor_tensor(h[i][:, BANK * jh : BANK * (jh + 1)], worse[i, jh][:], banks[i, jh][2][:], ALU.subtract)
+
+        def pick_front(i, m0, m1):
+            if m0 == 0:
+                front[i] = ring2.tile([P, NOTES], F32, name="front")
+            nc.vector.tensor_copy(front[i][:, m0:m1], h[i][:].indirect(pos1_sb[:, m0 // LIST : m1 // LIST]))
+
+        def pick_back(i, m0, m1):
+            b, t = divmod(i, PACK)
+            nc.vector.tensor_tensor(
+                zsum[b][:, t, m0:m1], h[i][:].indirect(pos2_sb[:, m0 // LIST : m1 // LIST]), front[i][:, m0:m1], ALU.add
+            )
+
+        def square_h(i):
+            b, t = divmod(i, PACK)
+            nc.scalar.activation(hsq[i][:], h[i][:], ACT.Square, scale=gh_sb[:, b, t : t + 1])
+
+        def weave_z(b, m0, m1, eng):
+            dst = zb[b][:, m0:m1, :].rearrange("p (c i) t -> p c t i", i=4)
+            src = zsum[b][:, :, m0:m1].rearrange("p t (c i) -> p c t i", i=4)
+            if eng == "act":
+                nc.scalar.copy(dst, src)
+            else:
+                nc.vector.tensor_copy(dst, src)
+
+        def quant_z(b, m0, m1):
+            nc.vector.quantize_mx(
+                out=zq[b][:, m0:m1].bitcast(FP8X4), scales=zs[b][:, m0:m1],
+                in_=zb[b][:, m0:m1, :].rearrange("p m t -> p (m t)"),
+            )
+
+        for i in range(TILES):
+            products(i, 0)
+            products(i, 1)
+            take_max(i, 0)
+            take_max(i, 1)
+            if i > 0:
+                pick_front(i - 1, 0, NOTES)
+            take_diff(i, 0)
+            if i > 0:
+                pick_back(i - 1, 0, NOTES)
+            take_diff(i, 1)
+            if i == 0:
+                cast(0, 1, 0, "act")
+                cast(0, 1, 1, "act")
+            if i == 1:
+                quant(0, 1)
+                cast(1, 1, 0, "act")
+                cast(1, 1, 1, "act")
+            if i == 2:
+                quant(1, 1)
+                deal_w3(1)
+                deal_w4s()
+            if i == 3:
+                deal_w4(0)
+            if i == 4:
+                weave_z(0, 0, NOTES, "act")
+            if i == 5:
+                quant_z(0, 0, NOTES)
+                deal_w4(1)
+            if i > 0:
+                square_h(i - 1)
+        last = TILES - 1
+        half = NOTES // 2
+        pick_front(last, 0, half)
+        pick_front(last, half, NOTES)
+        pick_back(last, 0, half)
+        weave_z(1, 0, half, "act")
+        pick_back(last, half, NOTES)
+        quant_z(1, 0, half)
+        weave_z(1, half, NOTES, "dve")
+        quant_z(1, half, NOTES)
+
+        y = {}
+        up = {}
+        out_rows = out.rearrange("(b p t) j -> b t p j", b=2, t=PACK)
+
+        def second(i):
+            c = slice(P * i, P * (i + 1))
+            py = psum.tile([P, BANK], F32, name="py")
+            nc.tensor.matmul_mx(
+                out=py[:], lhsT=w4w[0][:, c].bitcast(FP8X4), lhsT_scale=w4s[:, c],
+                rhs=zq[0][:].bitcast(FP8X4), rhs_scale=zs[0][:], start=True, stop=False,
+            )
+            parts = ((0, half), (half, NOTES)) if i == 0 else ((0, NOTES),)
+            for m0, m1 in parts:
+                nc.tensor.matmul_mx(
+                    out=py[:, m0:m1], lhsT=w4w[1][:, c].bitcast(FP8X4), lhsT_scale=w4s[4:P, c],
+                    rhs=zq[1][:, m0:m1].bitcast(FP8X4), rhs_scale=zs[1][:, m0:m1], start=False, stop=(m1 == NOTES),
+                )
+            y[i] = ring3.tile([P, NOTES], F32, name="y")
+            nc.scalar.copy(y[i][:], py[:])
+
+        quarter = S // 4
+
+        def pick_up(i, q):
+            if q == 0:
+                up[i] = ring3.tile([P, S], F32, name="up")
+            j0, j1 = quarter * q, quarter * (q + 1)
+            nc.vector.tensor_copy(up[i][:, j0:j1], y[i][:].indirect(pos3_sb[:, j0 // LIST : j1 // LIST]))
+
+        def square_up(i, j0, j1):
+            nc.scalar.activation(up[i][:, j0:j1], up[i][:, j0:j1], ACT.Square)
+
+        def add_up(i, j0, j1):
+            nc.vector.tensor_tensor(hsq[i][:, j0:j1], hsq[i][:, j0:j1], up[i][:, j0:j1], ALU.add)
+
+        def finish(i, j0, j1):
+            b, t = divmod(i, PACK)
+            nc.scalar.activation(hsq[i][:, j0:j1], hsq[i][:, j0:j1], ACT.Sqrt)
+            nc.sync.dma_start(out_rows[b, t][:, j0:j1], hsq[i][:, j0:j1])
+
+        second(0)
+        second(1)
+        square_h(last)
+        for i in range(last):
+            for q in range(4):
+                pick_up(i, q)
+            if i + 2 < TILES:
+                second(i + 2)
+            square_up(i, 0, S)
+            if i > 0:
+                add_up(i - 1, 0, S)
+                finish(i - 1, 0, S)
+        pick_up(last, 0)
+        square_up(last, 0, quarter)
+        pick_up(last, 1)
+        square_up(last, quarter, 2 * quarter)
+        add_up(last - 1, 0, S)
+        finish(last - 1, 0, S)
+        for q in range(4):
+            if q + 2 < 4:
+                pick_up(last, q + 2)
+                square_up(last, quarter * (q + 2), quarter * (q + 3))
+            add_up(last, quarter * q, quarter * (q + 1))
+            finish(last, quarter * q, quarter * (q + 1))

@@ -265,6 +265,9 @@ def tile_list_note_soiling_grade_kernel(
 
         y = {}
         up = {}
+        ywin = [keep.tile([P, NOTES + 32], F32, name="ywin%d" % r) for r in range(4)]
+        for r in range(4):
+            nc.gpsimd.memset(ywin[r][:, NOTES : NOTES + 32], 0.0)
         out_rows = out.rearrange("(b p t) j -> b t p j", b=2, t=PACK)
 
         def second(i):
@@ -280,22 +283,25 @@ def tile_list_note_soiling_grade_kernel(
                     out=py[:, m0:m1], lhsT=w4w[1][:, c].bitcast(FP8X4), lhsT_scale=w4s[4:P, c],
                     rhs=zq[1][:, m0:m1].bitcast(FP8X4), rhs_scale=zs[1][:, m0:m1], start=False, stop=(m1 == NOTES),
                 )
-            y[i] = ring3.tile([P, NOTES], F32, name="y")
-            nc.scalar.copy(y[i][:], py[:])
+            y[i] = ywin[i % 4]
+            if i in (2, 4, 6):
+                nc.vector.tensor_copy(y[i][:, 0:NOTES], py[:])
+            else:
+                nc.scalar.copy(y[i][:, 0:NOTES], py[:])
 
         quarter = S // 4
 
-        def pick_up(i, q):
-            if q == 0:
+        def pick_up(i, j0, j1):
+            if j0 == 0:
                 up[i] = ring3.tile([P, S], F32, name="up")
-            j0, j1 = quarter * q, quarter * (q + 1)
             nc.vector.tensor_copy(up[i][:, j0:j1], y[i][:].indirect(pos3_sb[:, j0 // LIST : j1 // LIST]))
 
         def square_up(i, j0, j1):
             nc.scalar.activation(up[i][:, j0:j1], up[i][:, j0:j1], ACT.Square)
 
         def add_up(i, j0, j1):
-            nc.vector.tensor_tensor(hsq[i][:, j0:j1], hsq[i][:, j0:j1], up[i][:, j0:j1], ALU.add)
+            eng = nc.vector if i == last else nc.gpsimd
+            eng.tensor_tensor(hsq[i][:, j0:j1], hsq[i][:, j0:j1], up[i][:, j0:j1], ALU.add)
 
         def finish(i, j0, j1):
             b, t = divmod(i, PACK)
@@ -306,23 +312,22 @@ def tile_list_note_soiling_grade_kernel(
         second(1)
         square_h(last)
         for i in range(last):
-            for q in range(4):
-                pick_up(i, q)
+            pick_up(i, 0, S // 2)
+            pick_up(i, S // 2, S)
             if i + 2 < TILES:
                 second(i + 2)
             square_up(i, 0, S)
+            add_up(i, 0, S)
             if i > 0:
-                add_up(i - 1, 0, S)
                 finish(i - 1, 0, S)
-        pick_up(last, 0)
+        pick_up(last, 0, quarter)
         square_up(last, 0, quarter)
-        pick_up(last, 1)
+        pick_up(last, quarter, 2 * quarter)
         square_up(last, quarter, 2 * quarter)
-        add_up(last - 1, 0, S)
         finish(last - 1, 0, S)
         for q in range(4):
             if q + 2 < 4:
-                pick_up(last, q + 2)
+                pick_up(last, quarter * (q + 2), quarter * (q + 3))
                 square_up(last, quarter * (q + 2), quarter * (q + 3))
             add_up(last, quarter * q, quarter * (q + 1))
             finish(last, quarter * q, quarter * (q + 1))

@@ -22,6 +22,10 @@ PASS = P * PACK
 BANK = 512
 TILES = H // P
 LIST = 16
+SUM_ON_VECTOR_FROM = 7168
+ROOT_LAG = 1536
+DIFF_ON_VECTOR = (0, 3, 7)
+Y_ON_VECTOR = (6, 7)
 
 
 def tile_list_note_soiling_grade_kernel(
@@ -30,9 +34,14 @@ def tile_list_note_soiling_grade_kernel(
     nc = tc.nc
     with ExitStack() as ctx:
         keep = ctx.enter_context(tc.tile_pool(name="keep", bufs=1))
-        ring2 = ctx.enter_context(tc.tile_pool(name="ring2", bufs=2))
-        ring3 = ctx.enter_context(tc.tile_pool(name="ring3", bufs=3))
-        psum = ctx.enter_context(tc.psum_pool(name="psum", bufs=2))
+        psum = ctx.enter_context(tc.psum_pool(name="psum", bufs=1))
+        bank = [psum.tile([P, BANK], F32, name="bank%d" % k) for k in range(8)]
+        grouped_ring = [keep.tile([P, PACK, P, PACK], BF16, name="grouped%d" % k, align_bytes=64) for k in range(2)]
+        work_ring = [keep.tile([P, S + S // 4], F32, name="work%d" % k) for k in range(2)]
+        worse_ring = [keep.tile([P, BANK], F32, name="worse%d" % k) for k in range(4)]
+        clean_ring = [keep.tile([P, BANK], F32, name="clean%d" % k) for k in range(3)]
+        h_ring = [keep.tile([P, S], F32, name="h%d" % k) for k in range(5)]
+        up_ring = [keep.tile([P, S], F32, name="up%d" % k) for k in range(3)]
 
         offs_sb = keep.tile([P, S // LIST], U16, name="offs_sb")
         pos1_sb = keep.tile([P, NOTES // LIST], U16, name="pos1_sb")
@@ -52,7 +61,8 @@ def tile_list_note_soiling_grade_kernel(
                 for mh in range(2):
                     raw[wi, b, mh] = keep.tile([P, PACK, 256], F32, name="raw%d%d%d" % (wi, b, mh), align_bytes=64)
 
-        nc.vector.memset(tabs[:].bitcast(I32), 0)
+        nc.gpsimd.memset(tabs[:, 0 : T // 2].bitcast(I32), 0)
+        nc.vector.memset(tabs[:, T // 2 : T].bitcast(I32), 0)
         nc.gpsimd.memset(w3s_raw[:].bitcast(I32), 0)
         nc.gpsimd.memset(w4s_raw[:].bitcast(I32), 0)
 
@@ -63,13 +73,13 @@ def tile_list_note_soiling_grade_kernel(
 
         nc.sync.dma_start(offs_sb[:], offs)
         load_raw(0, 0, 0)
-        for q in range(4):
-            nc.sync.dma_start(tabs[32 * q : 32 * q + 4, :].bitcast(I32), tab_scales[0, 4 * q : 4 * q + 4, :].bitcast(I32))
+        for r in range(4):
+            nc.sync.dma_start(tabs[r:P:32, :].bitcast(I32), tab_scales[0, r:16:4, :].bitcast(I32))
         load_raw(0, 0, 1)
-        nc.sync.dma_start(tabw[:], tab_words[0].rearrange("p t i -> p (t i)").bitcast(I32))
-        for q in range(4):
-            nc.sync.dma_start(w3s_raw[32 * q : 32 * q + 4, :].bitcast(I32), w3_scales[0, 4 * q : 4 * q + 4, :].bitcast(I32))
         nc.sync.dma_start(w3w_raw[:].bitcast(I32), w3_words[0].bitcast(I32))
+        nc.sync.dma_start(tabw[:], tab_words[0].rearrange("p t i -> p (t i)").bitcast(I32))
+        for r in range(4):
+            nc.sync.dma_start(w3s_raw[r:P:32, :].bitcast(I32), w3_scales[0, r:16:4, :].bitcast(I32))
         load_raw(1, 0, 0)
         load_raw(1, 0, 1)
         nc.sync.dma_start(pos1_sb[:], pos1)
@@ -84,11 +94,9 @@ def tile_list_note_soiling_grade_kernel(
             nc.sync.dma_start(w4s_raw[32 * q : 32 * q + 8, :].bitcast(I32), w4_scales[:, 4 * q : 4 * q + 4, :].bitcast(I32))
         nc.sync.dma_start(pos3_sb[:], pos3)
 
-        vw = [keep.tile([P, BANK], U32, name="vw%d" % jh, align_bytes=64) for jh in range(2)]
-        vs = [keep.tile([P, BANK], U8, name="vs%d" % jh, align_bytes=64) for jh in range(2)]
-        cols = BANK // LIST
-        for jh in range(2):
-            nc.vector.tensor_copy(vs[jh][:], tabs[:].indirect(offs_sb[:, jh * cols : (jh + 1) * cols]))
+        vw = keep.tile([P, S], U32, name="vw", align_bytes=64)
+        vs = keep.tile([P, S], U8, name="vs", align_bytes=64)
+        nc.vector.tensor_copy(vs[:], tabs[:].indirect(offs_sb[:]))
 
         grouped = {}
         wq = {}
@@ -96,21 +104,24 @@ def tile_list_note_soiling_grade_kernel(
 
         def cast(wi, b, mh, eng):
             if (wi, b) not in grouped:
-                grouped[wi, b] = ring2.tile([P, PACK, P, PACK], BF16, name="grouped", align_bytes=64)
+                grouped[wi, b] = grouped_ring[wi]
             dst = grouped[wi, b][:, :, 64 * mh : 64 * (mh + 1), :].rearrange("p t m j -> p m j t")
             src = raw[wi, b, mh][:].rearrange("p j (m t) -> p m j t", t=PACK)
             if eng == "act":
                 nc.scalar.copy(dst, src)
+            elif eng == "pool":
+                nc.gpsimd.tensor_copy(dst.rearrange("p m j t -> p t m j"), src.rearrange("p m j t -> p t m j"))
             else:
                 nc.vector.tensor_copy(dst, src)
 
-        def quant(wi, b):
-            wq[wi, b] = keep.tile([P, PASS], U32, name="wq%d%d" % (wi, b), align_bytes=64)
-            ws[wi, b] = keep.tile([P, PASS], U8, name="ws%d%d" % (wi, b), align_bytes=64)
+        def quant(wi, b, t0=0, t1=PACK):
+            if t0 == 0:
+                wq[wi, b] = keep.tile([P, PASS], U32, name="wq%d%d" % (wi, b), align_bytes=64)
+                ws[wi, b] = keep.tile([P, PASS], U8, name="ws%d%d" % (wi, b), align_bytes=64)
             nc.vector.quantize_mx(
-                out=wq[wi, b][:].bitcast(FP8X4),
-                scales=ws[wi, b][:],
-                in_=grouped[wi, b][:].rearrange("p t m j -> p (t m j)"),
+                out=wq[wi, b][:, P * t0 : P * t1].bitcast(FP8X4),
+                scales=ws[wi, b][:, P * t0 : P * t1],
+                in_=grouped[wi, b][:, t0:t1].rearrange("p t m j -> p (t m j)"),
             )
 
         w3w = [keep.tile([P, 2 * PASS], U8, name="w3w%d" % b, align_bytes=64) for b in range(2)]
@@ -128,13 +139,15 @@ def tile_list_note_soiling_grade_kernel(
 
         cast(0, 0, 0, "act")
         cast(0, 0, 1, "act")
+        deal_w3(0)
+        deal_w3(1)
         quant(0, 0)
         for jh in range(2):
-            nc.vector.tensor_copy(vw[jh][:], tabw[:].bitcast(U32).indirect(offs_sb[:, jh * cols : (jh + 1) * cols]))
+            picks = offs_sb[:, jh * BANK // LIST : (jh + 1) * BANK // LIST]
+            nc.vector.tensor_copy(vw[:, BANK * jh : BANK * (jh + 1)], tabw[:].bitcast(U32).indirect(picks))
         cast(1, 0, 0, "act")
         cast(1, 0, 1, "dve")
-        quant(1, 0)
-        deal_w3(0)
+        quant(1, 0, 0, 1)
 
         w4w = [keep.tile([P, H], U32, name="w4w%d" % a, align_bytes=64) for a in range(2)]
         w4s = keep.tile([P, H], U8, name="w4s", align_bytes=64)
@@ -161,47 +174,67 @@ def tile_list_note_soiling_grade_kernel(
         banks = {}
         worse = {}
         front = {}
+        work = {}
 
         def products(i, jh):
             b, t = divmod(i, PACK)
             c = slice(P * t, P * (t + 1))
-            pa = psum.tile([P, BANK], F32, name="pa")
-            pb = psum.tile([P, BANK], F32, name="pb")
-            pc = psum.tile([P, BANK], F32, name="pc")
-            rhs = vw[jh][:].bitcast(FP8X4)
+            pa, pb, pc = bank[2 + jh], bank[4 + jh], bank[6 + jh]
+            rhs = vw[:, BANK * jh : BANK * (jh + 1)].bitcast(FP8X4)
+            rhs_scale = vs[:, BANK * jh : BANK * (jh + 1)]
             for acc, wi in ((pa, 0), (pb, 1)):
                 nc.tensor.matmul_mx(
                     out=acc[:], lhsT=wq[wi, b][:, c].bitcast(FP8X4), lhsT_scale=ws[wi, b][:, c],
-                    rhs=rhs, rhs_scale=vs[jh][:], start=True, stop=True,
+                    rhs=rhs, rhs_scale=rhs_scale, start=True, stop=True,
                 )
             nc.tensor.matmul_mx(
                 out=pc[:], lhsT=w3w[b][:, 2 * P * t : 2 * P * (t + 1)].bitcast(FP4X4), lhsT_scale=w3s[b][:, c],
-                rhs=rhs, rhs_scale=vs[jh][:], start=True, stop=True,
+                rhs=rhs, rhs_scale=rhs_scale, start=True, stop=True,
             )
-            stain = ring3.tile([P, BANK], F32, name="stain")
-            nc.scalar.copy(stain[:], pa[:])
-            banks[i, jh] = (stain, pb, pc)
+            if jh == 0:
+                if i == 0:
+                    work[i] = raw[1, 0, 0][:].rearrange("p j c -> p (j c)")
+                else:
+                    work[i] = work_ring[i % len(work_ring)][:]
+            stain = work[i][:, BANK * jh : BANK * (jh + 1)]
+            nc.scalar.copy(stain, pa[:])
+            clean = pc[:]
+            if i not in DIFF_ON_VECTOR:
+                if jh == 0:
+                    clean = clean_ring[i % len(clean_ring)][:]
+                else:
+                    clean = zsum[(i - 1) // PACK][:, (i - 1) % PACK, :]
+                nc.scalar.copy(clean, pc[:])
+            banks[i, jh] = (stain, pb, clean)
 
         def take_max(i, jh):
             stain, pb, pc = banks[i, jh]
-            worse[i, jh] = ring3.tile([P, BANK], F32, name="worse")
-            nc.vector.tensor_tensor(worse[i, jh][:], pb[:], stain[:], ALU.max)
+            worse[i, jh] = worse_ring[(2 * i + jh) % len(worse_ring)]
+            nc.vector.tensor_tensor(worse[i, jh][:], pb[:], stain, ALU.max)
 
         def take_diff(i, jh):
             if jh == 0:
-                h[i] = ring3.tile([P, S], F32, name="h")
-            nc.vector.tensor_tensor(h[i][:, BANK * jh : BANK * (jh + 1)], worse[i, jh][:], banks[i, jh][2][:], ALU.subtract)
+                h[i] = h_ring[i % len(h_ring)]
+            dst = h[i][:, BANK * jh : BANK * (jh + 1)]
+            eng = nc.vector if i in DIFF_ON_VECTOR else nc.gpsimd
+            eng.tensor_tensor(dst, worse[i, jh][:], banks[i, jh][2], ALU.subtract)
 
         def pick_front(i, m0, m1):
-            if m0 == 0:
-                front[i] = ring2.tile([P, NOTES], F32, name="front")
+            if i + 1 < TILES:
+                front[i] = work[i + 1][:, S // 4 : 3 * S // 4]
+            elif m0 == 0:
+                front[i] = clean_ring[i % len(clean_ring)][:]
             nc.vector.tensor_copy(front[i][:, m0:m1], h[i][:].indirect(pos1_sb[:, m0 // LIST : m1 // LIST]))
 
         def pick_back(i, m0, m1):
             b, t = divmod(i, PACK)
-            nc.vector.tensor_tensor(
-                zsum[b][:, t, m0:m1], h[i][:].indirect(pos2_sb[:, m0 // LIST : m1 // LIST]), front[i][:, m0:m1], ALU.add
-            )
+            picked = h[i][:].indirect(pos2_sb[:, m0 // LIST : m1 // LIST])
+            if i == TILES - 1:
+                nc.vector.tensor_tensor(zsum[b][:, t, m0:m1], picked, front[i][:, m0:m1], ALU.add)
+            else:
+                back = work[i + 1][:, 3 * S // 4 : 5 * S // 4]
+                nc.vector.tensor_copy(back, picked)
+                nc.gpsimd.tensor_tensor(zsum[b][:, t, :], back, front[i], ALU.add)
 
         def square_h(i):
             b, t = divmod(i, PACK)
@@ -221,86 +254,94 @@ def tile_list_note_soiling_grade_kernel(
                 in_=zb[b][:, m0:m1, :].rearrange("p m t -> p (m t)"),
             )
 
+        products(0, 0)
+        products(0, 1)
         for i in range(TILES):
-            products(i, 0)
-            products(i, 1)
             take_max(i, 0)
+            if i == 0:
+                quant(1, 0, 1, PACK)
             take_max(i, 1)
+            take_diff(i, 0)
+            take_diff(i, 1)
+            if i == 3:
+                quant(1, 1)
+            if i + 1 < TILES:
+                products(i + 1, 0)
+                products(i + 1, 1)
             if i > 0:
                 pick_front(i - 1, 0, NOTES)
-            take_diff(i, 0)
-            if i > 0:
                 pick_back(i - 1, 0, NOTES)
-            take_diff(i, 1)
             if i == 0:
                 cast(0, 1, 0, "act")
                 cast(0, 1, 1, "act")
             if i == 1:
-                quant(0, 1)
                 cast(1, 1, 0, "act")
+            if i == 2:
                 cast(1, 1, 1, "act")
             if i == 2:
-                quant(1, 1)
-                deal_w3(1)
-                deal_w4s()
-            if i == 3:
-                deal_w4(0)
-            if i == 4:
-                weave_z(0, 0, NOTES, "act")
+                quant(0, 1)
             if i == 5:
-                quant_z(0, 0, NOTES)
+                deal_w4(0)
+            if i == 6:
                 deal_w4(1)
-            if i > 0:
+            if i == 3:
+                deal_w4s()
+            if i == 5:
+                weave_z(0, 0, NOTES // 2, "act")
+            if i == 6:
+                weave_z(0, NOTES // 2, NOTES, "act")
+            if i == 7:
+                quant_z(0, 0, NOTES)
+            if 0 < i < 5:
                 square_h(i - 1)
         last = TILES - 1
         half = NOTES // 2
+        for i in range(4, last):
+            square_h(i)
         pick_front(last, 0, half)
         pick_front(last, half, NOTES)
         pick_back(last, 0, half)
         weave_z(1, 0, half, "act")
         pick_back(last, half, NOTES)
-        quant_z(1, 0, half)
         weave_z(1, half, NOTES, "dve")
-        quant_z(1, half, NOTES)
+        quant_z(1, 0, NOTES)
 
         y = {}
         up = {}
-        ywin = [keep.tile([P, NOTES + 32], F32, name="ywin%d" % r) for r in range(4)]
-        for r in range(4):
+        ywin = [keep.tile([P, NOTES + 32], F32, name="ywin%d" % r) for r in range(TILES)]
+        for r in range(TILES):
             nc.gpsimd.memset(ywin[r][:, NOTES : NOTES + 32], 0.0)
         out_rows = out.rearrange("(b p t) j -> b t p j", b=2, t=PACK)
 
         def second(i):
             c = slice(P * i, P * (i + 1))
-            py = psum.tile([P, BANK], F32, name="py")
+            py = bank[i]
             nc.tensor.matmul_mx(
                 out=py[:], lhsT=w4w[0][:, c].bitcast(FP8X4), lhsT_scale=w4s[:, c],
                 rhs=zq[0][:].bitcast(FP8X4), rhs_scale=zs[0][:], start=True, stop=False,
             )
-            parts = ((0, half), (half, NOTES)) if i == 0 else ((0, NOTES),)
-            for m0, m1 in parts:
-                nc.tensor.matmul_mx(
-                    out=py[:, m0:m1], lhsT=w4w[1][:, c].bitcast(FP8X4), lhsT_scale=w4s[4:P, c],
-                    rhs=zq[1][:, m0:m1].bitcast(FP8X4), rhs_scale=zs[1][:, m0:m1], start=False, stop=(m1 == NOTES),
-                )
-            y[i] = ywin[i % 4]
-            if i in (2, 4, 6):
-                nc.vector.tensor_copy(y[i][:, 0:NOTES], py[:])
-            else:
-                nc.scalar.copy(y[i][:, 0:NOTES], py[:])
+            nc.tensor.matmul_mx(
+                out=py[:], lhsT=w4w[1][:, c].bitcast(FP8X4), lhsT_scale=w4s[4:P, c],
+                rhs=zq[1][:].bitcast(FP8X4), rhs_scale=zs[1][:], start=False, stop=True,
+            )
+            y[i] = py
 
-        quarter = S // 4
+        def fetch_y(i):
+            if i in Y_ON_VECTOR:
+                nc.vector.tensor_copy(ywin[i][:, 0:NOTES], y[i][:])
+            else:
+                nc.scalar.copy(ywin[i][:, 0:NOTES], y[i][:])
 
         def pick_up(i, j0, j1):
             if j0 == 0:
-                up[i] = ring3.tile([P, S], F32, name="up")
-            nc.vector.tensor_copy(up[i][:, j0:j1], y[i][:].indirect(pos3_sb[:, j0 // LIST : j1 // LIST]))
+                up[i] = up_ring[i % len(up_ring)]
+            nc.vector.tensor_copy(up[i][:, j0:j1], ywin[i][:].indirect(pos3_sb[:, j0 // LIST : j1 // LIST]))
 
         def square_up(i, j0, j1):
             nc.scalar.activation(up[i][:, j0:j1], up[i][:, j0:j1], ACT.Square)
 
         def add_up(i, j0, j1):
-            eng = nc.vector if i == last else nc.gpsimd
+            eng = nc.vector if S * i + j0 >= SUM_ON_VECTOR_FROM else nc.gpsimd
             eng.tensor_tensor(hsq[i][:, j0:j1], hsq[i][:, j0:j1], up[i][:, j0:j1], ALU.add)
 
         def finish(i, j0, j1):
@@ -308,26 +349,28 @@ def tile_list_note_soiling_grade_kernel(
             nc.scalar.activation(hsq[i][:, j0:j1], hsq[i][:, j0:j1], ACT.Sqrt)
             nc.sync.dma_start(out_rows[b, t][:, j0:j1], hsq[i][:, j0:j1])
 
-        second(0)
-        second(1)
+        def cuts(i):
+            n = (2,1,1,1,1,1,2,4)[i]
+            return [(S // n * k, S // n * (k + 1)) for k in range(n)]
+
+        for i in range(TILES):
+            second(i)
         square_h(last)
-        for i in range(last):
-            pick_up(i, 0, S // 2)
-            pick_up(i, S // 2, S)
-            if i + 2 < TILES:
-                second(i + 2)
-            square_up(i, 0, S)
-            add_up(i, 0, S)
-            if i > 0:
-                finish(i - 1, 0, S)
-        pick_up(last, 0, quarter)
-        square_up(last, 0, quarter)
-        pick_up(last, quarter, 2 * quarter)
-        square_up(last, quarter, 2 * quarter)
-        finish(last - 1, 0, S)
-        for q in range(4):
-            if q + 2 < 4:
-                pick_up(last, quarter * (q + 2), quarter * (q + 3))
-                square_up(last, quarter * (q + 2), quarter * (q + 3))
-            add_up(last, quarter * q, quarter * (q + 1))
-            finish(last, quarter * q, quarter * (q + 1))
+        for i in range(3):
+            fetch_y(i)
+        pending = []
+        for i in range(TILES):
+            for j0, j1 in cuts(i):
+                for g0 in range(j0, j1, BANK):
+                    pick_up(i, g0, min(g0 + BANK, j1))
+                square_up(i, j0, j1)
+                add_up(i, j0, j1)
+                if j0 == 0 and i + 3 < TILES:
+                    fetch_y(i + 3)
+                pending.append((i, j0, j1))
+                if i == 0 and j0 > 0:
+                    finish(*pending.pop(0))
+                while S * i + j1 - (S * pending[0][0] + pending[0][2]) >= ROOT_LAG:
+                    finish(*pending.pop(0))
+        for piece in pending:
+            finish(*piece)

@@ -21,11 +21,16 @@ PACK = 4
 PASS = P * PACK
 BANK = 512
 TILES = H // P
-LIST = 16
-SUM_ON_VECTOR_FROM = 7168
-ROOT_LAG = 1536
-DIFF_ON_VECTOR = (0, 3, 7)
-Y_ON_VECTOR = (6, 7)
+LAST = TILES - 1
+PER_COLUMN = 16
+W_PIECE = PASS // 2
+QUADRANT = 32
+SPARE = 32
+
+QUANTISE_STEP = PACK - 1
+DIFF_ON_VECTOR = (0, QUANTISE_STEP, LAST)
+PIECES = (2, 1, 1, 1, 1, 1, 2, 4)
+Y_AHEAD = 3
 
 
 def tile_list_note_soiling_grade_kernel(
@@ -35,18 +40,22 @@ def tile_list_note_soiling_grade_kernel(
     with ExitStack() as ctx:
         keep = ctx.enter_context(tc.tile_pool(name="keep", bufs=1))
         psum = ctx.enter_context(tc.psum_pool(name="psum", bufs=1))
-        bank = [psum.tile([P, BANK], F32, name="bank%d" % k) for k in range(8)]
-        grouped_ring = [keep.tile([P, PACK, P, PACK], BF16, name="grouped%d" % k, align_bytes=64) for k in range(2)]
-        work_ring = [keep.tile([P, S + S // 4], F32, name="work%d" % k) for k in range(2)]
-        worse_ring = [keep.tile([P, BANK], F32, name="worse%d" % k) for k in range(4)]
-        clean_ring = [keep.tile([P, BANK], F32, name="clean%d" % k) for k in range(3)]
-        h_ring = [keep.tile([P, S], F32, name="h%d" % k) for k in range(5)]
-        up_ring = [keep.tile([P, S], F32, name="up%d" % k) for k in range(3)]
+        bank = [psum.tile([P, BANK], F32, name="bank%d" % n) for n in range(8)]
+        stain_bank, crease_bank, clean_bank = bank[2:4], bank[4:6], bank[6:8]
 
-        offs_sb = keep.tile([P, S // LIST], U16, name="offs_sb")
-        pos1_sb = keep.tile([P, NOTES // LIST], U16, name="pos1_sb")
-        pos2_sb = keep.tile([P, NOTES // LIST], U16, name="pos2_sb")
-        pos3_sb = keep.tile([P, S // LIST], U16, name="pos3_sb")
+        woven_w = [keep.tile([P, PACK, P, PACK], BF16, name="woven_w%d" % n, align_bytes=64) for n in range(2)]
+        stain_ring = [keep.tile([P, S], F32, name="stain%d" % n) for n in range(2)]
+        worse_ring = [keep.tile([P, BANK], F32, name="worse%d" % n) for n in range(4)]
+        clean_ring = [keep.tile([P, BANK], F32, name="clean%d" % n) for n in range(3)]
+        h_ring = [keep.tile([P, S], F32, name="h%d" % n) for n in range(5)]
+
+        offs_sb = keep.tile([P, S // PER_COLUMN], U16, name="offs_sb")
+        pos1_sb = keep.tile([P, NOTES // PER_COLUMN], U16, name="pos1_sb")
+        pos2_sb = keep.tile([P, NOTES // PER_COLUMN], U16, name="pos2_sb")
+        pos3_sb = keep.tile([P, S // PER_COLUMN], U16, name="pos3_sb")
+
+        def entries(lst, e0, e1):
+            return lst[:, e0 // PER_COLUMN : e1 // PER_COLUMN]
 
         tabw = keep.tile([P, T], I32, name="tabw", align_bytes=64)
         tabs = keep.tile([P, T], U8, name="tabs", align_bytes=64)
@@ -58,70 +67,75 @@ def tile_list_note_soiling_grade_kernel(
         raw = {}
         for wi in range(2):
             for b in range(2):
-                for mh in range(2):
-                    raw[wi, b, mh] = keep.tile([P, PACK, 256], F32, name="raw%d%d%d" % (wi, b, mh), align_bytes=64)
+                for piece in range(2):
+                    raw[wi, b, piece] = keep.tile(
+                        [P, PACK, W_PIECE], F32, name="raw%d%d%d" % (wi, b, piece), align_bytes=64
+                    )
+
+        def flat(tile):
+            return tile[:].rearrange("p j c -> p (j c)")
 
         nc.gpsimd.memset(tabs[:, 0 : T // 2].bitcast(I32), 0)
         nc.vector.memset(tabs[:, T // 2 : T].bitcast(I32), 0)
         nc.gpsimd.memset(w3s_raw[:].bitcast(I32), 0)
         nc.gpsimd.memset(w4s_raw[:].bitcast(I32), 0)
 
-        def load_raw(wi, b, mh):
-            w = (w1, w2)[wi]
-            c0 = PASS * b + 256 * mh
-            nc.sync.dma_start(raw[wi, b, mh][:], w[:, c0 : c0 + 256].rearrange("(p j) c -> p j c", j=PACK))
+        warm = keep.tile([P, 2], F32, name="warm")
+        nc.gpsimd.memset(warm[:, 0:1], 1.0)
+        nc.scalar.activation(warm[:, 1:2], warm[:, 0:1], ACT.Sqrt)
+
+        def load_raw(wi, b, piece):
+            c0 = PASS * b + W_PIECE * piece
+            rows = (w1, w2)[wi][:, c0 : c0 + W_PIECE]
+            nc.sync.dma_start(raw[wi, b, piece][:], rows.rearrange("(p j) c -> p j c", j=PACK))
+
+        def load_scale_rows(tile, rows):
+            for r in range(4):
+                nc.sync.dma_start(tile[r:P:QUADRANT, :].bitcast(I32), rows[r:16:4, :].bitcast(I32))
 
         nc.sync.dma_start(offs_sb[:], offs)
         load_raw(0, 0, 0)
-        for r in range(4):
-            nc.sync.dma_start(tabs[r:P:32, :].bitcast(I32), tab_scales[0, r:16:4, :].bitcast(I32))
+        load_scale_rows(tabs, tab_scales[0])
         load_raw(0, 0, 1)
         nc.sync.dma_start(w3w_raw[:].bitcast(I32), w3_words[0].bitcast(I32))
         nc.sync.dma_start(tabw[:], tab_words[0].rearrange("p t i -> p (t i)").bitcast(I32))
-        for r in range(4):
-            nc.sync.dma_start(w3s_raw[r:P:32, :].bitcast(I32), w3_scales[0, r:16:4, :].bitcast(I32))
+        load_scale_rows(w3s_raw, w3_scales[0])
         load_raw(1, 0, 0)
         load_raw(1, 0, 1)
         nc.sync.dma_start(pos1_sb[:], pos1)
         nc.sync.dma_start(pos2_sb[:], pos2)
         nc.sync.dma_start(gh_sb[:], gh.rearrange("(b p t) -> p b t", b=2, t=PACK))
         for wi in range(2):
-            for mh in range(2):
-                load_raw(wi, 1, mh)
+            for piece in range(2):
+                load_raw(wi, 1, piece)
         for a in range(2):
             nc.sync.dma_start(w4w_raw[a][:], w4_words[a].rearrange("p c i -> p (c i)").bitcast(I32))
         for q in range(4):
-            nc.sync.dma_start(w4s_raw[32 * q : 32 * q + 8, :].bitcast(I32), w4_scales[:, 4 * q : 4 * q + 4, :].bitcast(I32))
+            nc.sync.dma_start(
+                w4s_raw[QUADRANT * q : QUADRANT * q + 8, :].bitcast(I32), w4_scales[:, 4 * q : 4 * q + 4, :].bitcast(I32)
+            )
         nc.sync.dma_start(pos3_sb[:], pos3)
 
         vw = keep.tile([P, S], U32, name="vw", align_bytes=64)
         vs = keep.tile([P, S], U8, name="vs", align_bytes=64)
         nc.vector.tensor_copy(vs[:], tabs[:].indirect(offs_sb[:]))
 
-        grouped = {}
         wq = {}
         ws = {}
 
-        def cast(wi, b, mh, eng):
-            if (wi, b) not in grouped:
-                grouped[wi, b] = grouped_ring[wi]
-            dst = grouped[wi, b][:, :, 64 * mh : 64 * (mh + 1), :].rearrange("p t m j -> p m j t")
-            src = raw[wi, b, mh][:].rearrange("p j (m t) -> p m j t", t=PACK)
-            if eng == "act":
-                nc.scalar.copy(dst, src)
-            elif eng == "pool":
-                nc.gpsimd.tensor_copy(dst.rearrange("p m j t -> p t m j"), src.rearrange("p m j t -> p t m j"))
-            else:
-                nc.vector.tensor_copy(dst, src)
+        def weave_w(copy, wi, b, piece):
+            m0 = W_PIECE // PACK * piece
+            dst = woven_w[wi][:, :, m0 : m0 + W_PIECE // PACK, :].rearrange("p t m j -> p m j t")
+            copy(dst, raw[wi, b, piece][:].rearrange("p j (m t) -> p m j t", t=PACK))
 
-        def quant(wi, b, t0=0, t1=PACK):
+        def quantise_w(wi, b, t0, t1):
             if t0 == 0:
                 wq[wi, b] = keep.tile([P, PASS], U32, name="wq%d%d" % (wi, b), align_bytes=64)
                 ws[wi, b] = keep.tile([P, PASS], U8, name="ws%d%d" % (wi, b), align_bytes=64)
             nc.vector.quantize_mx(
                 out=wq[wi, b][:, P * t0 : P * t1].bitcast(FP8X4),
                 scales=ws[wi, b][:, P * t0 : P * t1],
-                in_=grouped[wi, b][:, t0:t1].rearrange("p t m j -> p (t m j)"),
+                in_=woven_w[wi][:, t0:t1].rearrange("p t m j -> p (t m j)"),
             )
 
         w3w = [keep.tile([P, 2 * PASS], U8, name="w3w%d" % b, align_bytes=64) for b in range(2)]
@@ -137,240 +151,200 @@ def tile_list_note_soiling_grade_kernel(
                 w3s_raw[:, PASS * b : PASS * (b + 1)].rearrange("p (m t) -> p t m", t=PACK),
             )
 
-        cast(0, 0, 0, "act")
-        cast(0, 0, 1, "act")
+        weave_w(nc.scalar.copy, 0, 0, 0)
+        weave_w(nc.scalar.copy, 0, 0, 1)
         deal_w3(0)
         deal_w3(1)
-        quant(0, 0)
-        for jh in range(2):
-            picks = offs_sb[:, jh * BANK // LIST : (jh + 1) * BANK // LIST]
-            nc.vector.tensor_copy(vw[:, BANK * jh : BANK * (jh + 1)], tabw[:].bitcast(U32).indirect(picks))
-        cast(1, 0, 0, "act")
-        cast(1, 0, 1, "dve")
-        quant(1, 0, 0, 1)
+        quantise_w(0, 0, 0, PACK)
+        for j0 in range(0, S, BANK):
+            nc.vector.tensor_copy(
+                vw[:, j0 : j0 + BANK], tabw[:].bitcast(U32).indirect(entries(offs_sb, j0, j0 + BANK))
+            )
+        weave_w(nc.scalar.copy, 1, 0, 0)
+        weave_w(nc.vector.tensor_copy, 1, 0, 1)
+        quantise_w(1, 0, 0, 1)
 
         w4w = [keep.tile([P, H], U32, name="w4w%d" % a, align_bytes=64) for a in range(2)]
         w4s = keep.tile([P, H], U8, name="w4s", align_bytes=64)
 
-        def deal_w4(a):
+        def deal_w4_words(a):
             for b in range(2):
                 nc.scalar.copy(
                     w4w[a][:, PASS * b : PASS * (b + 1)].rearrange("p (t m) -> p m t", t=PACK),
                     w4w_raw[a][:, PASS * b : PASS * (b + 1)].bitcast(U32).rearrange("p (m t) -> p m t", t=PACK),
                 )
 
-        def deal_w4s():
+        def deal_w4_scales():
             nc.gpsimd.tensor_copy(
                 w4s[:].rearrange("p (b t m) -> p b t m", b=2, t=PACK),
                 w4s_raw[:].rearrange("p (b m t) -> p b t m", b=2, t=PACK),
             )
 
-        hsq = [keep.tile([P, S], F32, name="hsq%d" % i) for i in range(TILES)]
-        zsum = [keep.tile([P, PACK, NOTES], F32, name="zsum%d" % b) for b in range(2)]
-        zb = [keep.tile([P, NOTES, PACK], BF16, name="zb%d" % b, align_bytes=64) for b in range(2)]
+        z = [keep.tile([P, PACK, NOTES], F32, name="z%d" % b) for b in range(2)]
+        acc = [keep.tile([P, S], F32, name="acc%d" % i)[:] for i in range(LAST)]
+        acc.append(z[1][:, 0:2, :].rearrange("p t m -> p (t m)"))
+        gh_last = gh_sb[:, 1, PACK - 1 : PACK]
+        gh_last_squared = keep.tile([P, 1], F32, name="gh_last_squared")
+        nc.gpsimd.tensor_tensor(gh_last_squared[:], gh_last, gh_last, ALU.mult)
+        woven_z = [keep.tile([P, NOTES, PACK], BF16, name="woven_z%d" % b, align_bytes=64) for b in range(2)]
         zq = [keep.tile([P, NOTES], U32, name="zq%d" % b, align_bytes=64) for b in range(2)]
         zs = [keep.tile([P, NOTES], U8, name="zs%d" % b, align_bytes=64) for b in range(2)]
-        h = {}
-        banks = {}
-        worse = {}
-        front = {}
-        work = {}
 
-        def products(i, jh):
+        def z_rows(i):
+            return z[i // PACK][:, i % PACK, :]
+
+        def half(ap, jh):
+            return ap[:, BANK * jh : BANK * (jh + 1)]
+
+        def stain_of(i):
+            return flat(raw[1, 0, 0]) if i == 0 else stain_ring[i % len(stain_ring)][:]
+
+        def clean_of(i, jh):
+            if i in DIFF_ON_VECTOR:
+                return clean_bank[jh][:]
+            return clean_ring[i % len(clean_ring)][:] if jh == 0 else z_rows(i - 1)
+
+        def worse_of(i, jh):
+            return worse_ring[(2 * i + jh) % len(worse_ring)][:]
+
+        def h_of(i):
+            return h_ring[i % len(h_ring)][:]
+
+        def product(into, words, scales, jh):
+            nc.tensor.matmul_mx(
+                out=into[:], lhsT=words, lhsT_scale=scales,
+                rhs=half(vw, jh).bitcast(FP8X4), rhs_scale=half(vs, jh), start=True, stop=True,
+            )
+
+        def products(i):
             b, t = divmod(i, PACK)
             c = slice(P * t, P * (t + 1))
-            pa, pb, pc = bank[2 + jh], bank[4 + jh], bank[6 + jh]
-            rhs = vw[:, BANK * jh : BANK * (jh + 1)].bitcast(FP8X4)
-            rhs_scale = vs[:, BANK * jh : BANK * (jh + 1)]
-            for acc, wi in ((pa, 0), (pb, 1)):
-                nc.tensor.matmul_mx(
-                    out=acc[:], lhsT=wq[wi, b][:, c].bitcast(FP8X4), lhsT_scale=ws[wi, b][:, c],
-                    rhs=rhs, rhs_scale=rhs_scale, start=True, stop=True,
-                )
-            nc.tensor.matmul_mx(
-                out=pc[:], lhsT=w3w[b][:, 2 * P * t : 2 * P * (t + 1)].bitcast(FP4X4), lhsT_scale=w3s[b][:, c],
-                rhs=rhs, rhs_scale=rhs_scale, start=True, stop=True,
-            )
-            if jh == 0:
-                if i == 0:
-                    work[i] = raw[1, 0, 0][:].rearrange("p j c -> p (j c)")
-                else:
-                    work[i] = work_ring[i % len(work_ring)][:]
-            stain = work[i][:, BANK * jh : BANK * (jh + 1)]
-            nc.scalar.copy(stain, pa[:])
-            clean = pc[:]
-            if i not in DIFF_ON_VECTOR:
-                if jh == 0:
-                    clean = clean_ring[i % len(clean_ring)][:]
-                else:
-                    clean = zsum[(i - 1) // PACK][:, (i - 1) % PACK, :]
-                nc.scalar.copy(clean, pc[:])
-            banks[i, jh] = (stain, pb, clean)
+            for jh in range(2):
+                product(stain_bank[jh], wq[0, b][:, c].bitcast(FP8X4), ws[0, b][:, c], jh)
+                nc.scalar.copy(half(stain_of(i), jh), stain_bank[jh][:])
+            for jh in range(2):
+                product(crease_bank[jh], wq[1, b][:, c].bitcast(FP8X4), ws[1, b][:, c], jh)
+                product(clean_bank[jh], w3w[b][:, 2 * P * t : 2 * P * (t + 1)].bitcast(FP4X4), w3s[b][:, c], jh)
+                if i not in DIFF_ON_VECTOR:
+                    nc.scalar.copy(clean_of(i, jh), clean_bank[jh][:])
 
         def take_max(i, jh):
-            stain, pb, pc = banks[i, jh]
-            worse[i, jh] = worse_ring[(2 * i + jh) % len(worse_ring)]
-            nc.vector.tensor_tensor(worse[i, jh][:], pb[:], stain, ALU.max)
+            nc.vector.tensor_tensor(worse_of(i, jh), crease_bank[jh][:], half(stain_of(i), jh), ALU.max)
 
         def take_diff(i, jh):
-            if jh == 0:
-                h[i] = h_ring[i % len(h_ring)]
-            dst = h[i][:, BANK * jh : BANK * (jh + 1)]
-            eng = nc.vector if i in DIFF_ON_VECTOR else nc.gpsimd
-            eng.tensor_tensor(dst, worse[i, jh][:], banks[i, jh][2], ALU.subtract)
+            engine = nc.vector if i in DIFF_ON_VECTOR else nc.gpsimd
+            engine.tensor_tensor(half(h_of(i), jh), worse_of(i, jh), clean_of(i, jh), ALU.subtract)
 
-        def pick_front(i, m0, m1):
-            if i + 1 < TILES:
-                front[i] = work[i + 1][:, S // 4 : 3 * S // 4]
-            elif m0 == 0:
-                front[i] = clean_ring[i % len(clean_ring)][:]
-            nc.vector.tensor_copy(front[i][:, m0:m1], h[i][:].indirect(pos1_sb[:, m0 // LIST : m1 // LIST]))
-
-        def pick_back(i, m0, m1):
-            b, t = divmod(i, PACK)
-            picked = h[i][:].indirect(pos2_sb[:, m0 // LIST : m1 // LIST])
-            if i == TILES - 1:
-                nc.vector.tensor_tensor(zsum[b][:, t, m0:m1], picked, front[i][:, m0:m1], ALU.add)
-            else:
-                back = work[i + 1][:, 3 * S // 4 : 5 * S // 4]
-                nc.vector.tensor_copy(back, picked)
-                nc.gpsimd.tensor_tensor(zsum[b][:, t, :], back, front[i], ALU.add)
+        def pair_up(i):
+            front, back = half(stain_of(i + 1), 0), half(stain_of(i + 1), 1)
+            nc.vector.tensor_copy(front, h_of(i).indirect(pos1_sb[:]))
+            nc.vector.tensor_copy(back, h_of(i).indirect(pos2_sb[:]))
+            nc.gpsimd.tensor_tensor(z_rows(i), back, front, ALU.add)
 
         def square_h(i):
             b, t = divmod(i, PACK)
-            nc.scalar.activation(hsq[i][:], h[i][:], ACT.Square, scale=gh_sb[:, b, t : t + 1])
+            nc.scalar.activation(acc[i], h_of(i), ACT.Square, scale=gh_sb[:, b, t : t + 1])
 
-        def weave_z(b, m0, m1, eng):
-            dst = zb[b][:, m0:m1, :].rearrange("p (c i) t -> p c t i", i=4)
-            src = zsum[b][:, :, m0:m1].rearrange("p t (c i) -> p c t i", i=4)
-            if eng == "act":
-                nc.scalar.copy(dst, src)
-            else:
-                nc.vector.tensor_copy(dst, src)
+        def weave_z(copy, b, m0, m1):
+            dst = woven_z[b][:, m0:m1, :].rearrange("p (c i) t -> p c t i", i=4)
+            copy(dst, z[b][:, :, m0:m1].rearrange("p t (c i) -> p c t i", i=4))
 
-        def quant_z(b, m0, m1):
+        def quantise_z(b):
             nc.vector.quantize_mx(
-                out=zq[b][:, m0:m1].bitcast(FP8X4), scales=zs[b][:, m0:m1],
-                in_=zb[b][:, m0:m1, :].rearrange("p m t -> p (m t)"),
+                out=zq[b][:].bitcast(FP8X4), scales=zs[b][:], in_=woven_z[b][:].rearrange("p m t -> p (m t)")
             )
 
-        products(0, 0)
-        products(0, 1)
+        mid = NOTES // 2
+        products(0)
         for i in range(TILES):
             take_max(i, 0)
             if i == 0:
-                quant(1, 0, 1, PACK)
+                quantise_w(1, 0, 1, PACK)
             take_max(i, 1)
             take_diff(i, 0)
             take_diff(i, 1)
-            if i == 3:
-                quant(1, 1)
-            if i + 1 < TILES:
-                products(i + 1, 0)
-                products(i + 1, 1)
+            if i == QUANTISE_STEP:
+                quantise_w(0, 1, 0, PACK)
+                quantise_w(1, 1, 0, PACK)
+            if i < LAST:
+                products(i + 1)
             if i > 0:
-                pick_front(i - 1, 0, NOTES)
-                pick_back(i - 1, 0, NOTES)
-            if i == 0:
-                cast(0, 1, 0, "act")
-                cast(0, 1, 1, "act")
-            if i == 1:
-                cast(1, 1, 0, "act")
-            if i == 2:
-                cast(1, 1, 1, "act")
-            if i == 2:
-                quant(0, 1)
-            if i == 5:
-                deal_w4(0)
-            if i == 6:
-                deal_w4(1)
-            if i == 3:
-                deal_w4s()
-            if i == 5:
-                weave_z(0, 0, NOTES // 2, "act")
-            if i == 6:
-                weave_z(0, NOTES // 2, NOTES, "act")
-            if i == 7:
-                quant_z(0, 0, NOTES)
-            if 0 < i < 5:
+                pair_up(i - 1)
+            if i < 2:
+                weave_w(nc.scalar.copy, i, 1, 0)
+            if i == QUANTISE_STEP - 1:
+                weave_w(nc.scalar.copy, 0, 1, 1)
+                weave_w(nc.scalar.copy, 1, 1, 1)
+            if i == QUANTISE_STEP:
+                deal_w4_scales()
+                for done in range(i):
+                    square_h(done)
+            if i == QUANTISE_STEP + 1:
                 square_h(i - 1)
-        last = TILES - 1
-        half = NOTES // 2
-        for i in range(4, last):
+            if i >= LAST - 1:
+                deal_w4_words(i - (LAST - 1))
+            if i in (LAST - 2, LAST - 1):
+                m0 = mid * (i - (LAST - 2))
+                weave_z(nc.scalar.copy, 0, m0, m0 + mid)
+        quantise_z(0)
+        for i in range(QUANTISE_STEP + 1, LAST - 1):
             square_h(i)
-        pick_front(last, 0, half)
-        pick_front(last, half, NOTES)
-        pick_back(last, 0, half)
-        weave_z(1, 0, half, "act")
-        pick_back(last, half, NOTES)
-        weave_z(1, half, NOTES, "dve")
-        quant_z(1, 0, NOTES)
 
-        y = {}
-        up = {}
-        ywin = [keep.tile([P, NOTES + 32], F32, name="ywin%d" % r) for r in range(TILES)]
-        for r in range(TILES):
-            nc.gpsimd.memset(ywin[r][:, NOTES : NOTES + 32], 0.0)
-        out_rows = out.rearrange("(b p t) j -> b t p j", b=2, t=PACK)
+        front = clean_ring[LAST % len(clean_ring)]
+        for m0 in (0, mid):
+            nc.vector.tensor_copy(front[:, m0 : m0 + mid], h_of(LAST).indirect(entries(pos1_sb, m0, m0 + mid)))
+        for m0, copy in ((0, nc.scalar.copy), (mid, nc.vector.tensor_copy)):
+            picked = h_of(LAST).indirect(entries(pos2_sb, m0, m0 + mid))
+            nc.vector.tensor_tensor(z_rows(LAST)[:, m0 : m0 + mid], picked, front[:, m0 : m0 + mid], ALU.add)
+            weave_z(copy, 1, m0, m0 + mid)
+        quantise_z(1)
+        square_h(LAST - 1)
+        nc.vector.scalar_tensor_tensor(acc[LAST], h_of(LAST), gh_last_squared[:], h_of(LAST), ALU.mult, ALU.mult)
 
-        def second(i):
+        y = [keep.tile([P, NOTES + SPARE], F32, name="y%d" % i) for i in range(TILES)]
+        for i in range(TILES):
+            nc.gpsimd.memset(y[i][:, NOTES : NOTES + SPARE], 0.0)
+        for i in range(TILES):
             c = slice(P * i, P * (i + 1))
-            py = bank[i]
-            nc.tensor.matmul_mx(
-                out=py[:], lhsT=w4w[0][:, c].bitcast(FP8X4), lhsT_scale=w4s[:, c],
-                rhs=zq[0][:].bitcast(FP8X4), rhs_scale=zs[0][:], start=True, stop=False,
-            )
-            nc.tensor.matmul_mx(
-                out=py[:], lhsT=w4w[1][:, c].bitcast(FP8X4), lhsT_scale=w4s[4:P, c],
-                rhs=zq[1][:].bitcast(FP8X4), rhs_scale=zs[1][:], start=False, stop=True,
-            )
-            y[i] = py
+            for a in range(2):
+                nc.tensor.matmul_mx(
+                    out=bank[i][:], lhsT=w4w[a][:, c].bitcast(FP8X4), lhsT_scale=w4s[4 * a : P, c],
+                    rhs=zq[a][:].bitcast(FP8X4), rhs_scale=zs[a][:], start=(a == 0), stop=(a == 1),
+                )
 
         def fetch_y(i):
-            if i in Y_ON_VECTOR:
-                nc.vector.tensor_copy(ywin[i][:, 0:NOTES], y[i][:])
-            else:
-                nc.scalar.copy(ywin[i][:, 0:NOTES], y[i][:])
+            nc.scalar.copy(y[i][:, 0:NOTES], bank[i][:])
 
-        def pick_up(i, j0, j1):
-            if j0 == 0:
-                up[i] = up_ring[i % len(up_ring)]
-            nc.vector.tensor_copy(up[i][:, j0:j1], ywin[i][:].indirect(pos3_sb[:, j0 // LIST : j1 // LIST]))
+        up_ring = [flat(raw[0, 0, 0]), flat(raw[0, 0, 1]), flat(raw[1, 0, 1])]
+        out_rows = out.rearrange("(b p t) j -> b t p j", b=2, t=PACK)
 
-        def square_up(i, j0, j1):
-            nc.scalar.activation(up[i][:, j0:j1], up[i][:, j0:j1], ACT.Square)
+        def pick_square_add(i, j0, j1):
+            up = up_ring[i % len(up_ring)]
+            for g0 in range(j0, j1, BANK):
+                g1 = min(g0 + BANK, j1)
+                nc.vector.tensor_copy(up[:, g0:g1], y[i][:].indirect(entries(pos3_sb, g0, g1)))
+            nc.scalar.activation(up[:, j0:j1], up[:, j0:j1], ACT.Square)
+            engine = nc.vector if i == LAST else nc.gpsimd
+            engine.tensor_tensor(acc[i][:, j0:j1], acc[i][:, j0:j1], up[:, j0:j1], ALU.add)
 
-        def add_up(i, j0, j1):
-            eng = nc.vector if S * i + j0 >= SUM_ON_VECTOR_FROM else nc.gpsimd
-            eng.tensor_tensor(hsq[i][:, j0:j1], hsq[i][:, j0:j1], up[i][:, j0:j1], ALU.add)
-
-        def finish(i, j0, j1):
+        def root_and_store(i, j0, j1):
             b, t = divmod(i, PACK)
-            nc.scalar.activation(hsq[i][:, j0:j1], hsq[i][:, j0:j1], ACT.Sqrt)
-            nc.sync.dma_start(out_rows[b, t][:, j0:j1], hsq[i][:, j0:j1])
+            nc.scalar.activation(acc[i][:, j0:j1], acc[i][:, j0:j1], ACT.Sqrt)
+            nc.sync.dma_start(out_rows[b, t][:, j0:j1], acc[i][:, j0:j1])
 
-        def cuts(i):
-            n = (2,1,1,1,1,1,2,4)[i]
-            return [(S // n * k, S // n * (k + 1)) for k in range(n)]
-
-        for i in range(TILES):
-            second(i)
-        square_h(last)
-        for i in range(3):
+        for i in range(Y_AHEAD):
             fetch_y(i)
+        fetch_behind = [range(3, 4), range(4, 7), range(7, 8)]
         pending = []
         for i in range(TILES):
-            for j0, j1 in cuts(i):
-                for g0 in range(j0, j1, BANK):
-                    pick_up(i, g0, min(g0 + BANK, j1))
-                square_up(i, j0, j1)
-                add_up(i, j0, j1)
-                if j0 == 0 and i + 3 < TILES:
-                    fetch_y(i + 3)
-                pending.append((i, j0, j1))
-                if i == 0 and j0 > 0:
-                    finish(*pending.pop(0))
-                while S * i + j1 - (S * pending[0][0] + pending[0][2]) >= ROOT_LAG:
-                    finish(*pending.pop(0))
+            width = S // PIECES[i]
+            for j0 in range(0, S, width):
+                pick_square_add(i, j0, j0 + width)
+                if fetch_behind:
+                    for later in fetch_behind.pop(0):
+                        fetch_y(later)
+                pending.append((i, j0, j0 + width))
+                while S * (i - pending[0][0]) + j0 + width - pending[0][2] >= S:
+                    root_and_store(*pending.pop(0))
         for piece in pending:
-            finish(*piece)
+            root_and_store(*piece)

from contextlib import ExitStack

import concourse.mybir as mybir

K, T, S, NOTES, H = 512, 4096, 1024, 512, 1024
FLOPS = 3 * 2 * K * H * S + 2 * H * H * NOTES

F32 = mybir.dt.float32
BF16 = mybir.dt.bfloat16
I32 = mybir.dt.int32
U32 = mybir.dt.uint32
U16 = mybir.dt.uint16
U8 = mybir.dt.uint8
FP8X4 = mybir.dt.float8_e4m3fn_x4
FP4X4 = mybir.dt.float4_e2m1fn_x4
ALU = mybir.AluOpType
ACT = mybir.ActivationFunctionType

P = 128
PACK = 4
PASS = P * PACK
BANK = 512
TILES = H // P
LAST = TILES - 1
PER_COLUMN = 16
W_PIECE = PASS // 2
QUADRANT = 32
SPARE = 32

QUANTISE_STEP = PACK - 1
DIFF_ON_VECTOR = (0, QUANTISE_STEP, LAST)
PIECES = (2, 1, 1, 1, 1, 1, 2, 4)
Y_AHEAD = 3


def tile_list_note_soiling_grade_kernel(
    tc, tab_words, tab_scales, offs, pos1, pos2, pos3, w1, w2, w3_words, w3_scales, w4_words, w4_scales, gh, out
):
    nc = tc.nc
    with ExitStack() as ctx:
        keep = ctx.enter_context(tc.tile_pool(name="keep", bufs=1))
        psum = ctx.enter_context(tc.psum_pool(name="psum", bufs=1))
        bank = [psum.tile([P, BANK], F32, name="bank%d" % n) for n in range(8)]
        stain_bank, crease_bank, clean_bank = bank[2:4], bank[4:6], bank[6:8]

        woven_w = [keep.tile([P, PACK, P, PACK], BF16, name="woven_w%d" % n, align_bytes=64) for n in range(2)]
        stain_ring = [keep.tile([P, S], F32, name="stain%d" % n) for n in range(2)]
        worse_ring = [keep.tile([P, BANK], F32, name="worse%d" % n) for n in range(4)]
        clean_ring = [keep.tile([P, BANK], F32, name="clean%d" % n) for n in range(3)]
        h_ring = [keep.tile([P, S], F32, name="h%d" % n) for n in range(5)]

        offs_sb = keep.tile([P, S // PER_COLUMN], U16, name="offs_sb")
        pos1_sb = keep.tile([P, NOTES // PER_COLUMN], U16, name="pos1_sb")
        pos2_sb = keep.tile([P, NOTES // PER_COLUMN], U16, name="pos2_sb")
        pos3_sb = keep.tile([P, S // PER_COLUMN], U16, name="pos3_sb")

        def entries(lst, e0, e1):
            return lst[:, e0 // PER_COLUMN : e1 // PER_COLUMN]

        tabw = keep.tile([P, T], I32, name="tabw", align_bytes=64)
        tabs = keep.tile([P, T], U8, name="tabs", align_bytes=64)
        w3w_raw = keep.tile([P, 2 * H], U8, name="w3w_raw", align_bytes=64)
        w3s_raw = keep.tile([P, H], U8, name="w3s_raw", align_bytes=64)
        w4s_raw = keep.tile([P, H], U8, name="w4s_raw", align_bytes=64)
        w4w_raw = [keep.tile([P, H], I32, name="w4w_raw%d" % a, align_bytes=64) for a in range(2)]
        gh_sb = keep.tile([P, 2, PACK], F32, name="gh_sb")
        raw = {}
        for wi in range(2):
            for b in range(2):
                for piece in range(2):
                    raw[wi, b, piece] = keep.tile(
                        [P, PACK, W_PIECE], F32, name="raw%d%d%d" % (wi, b, piece), align_bytes=64
                    )

        def flat(tile):
            return tile[:].rearrange("p j c -> p (j c)")

        nc.gpsimd.memset(tabs[:, 0 : T // 2].bitcast(I32), 0)
        nc.vector.memset(tabs[:, T // 2 : T].bitcast(I32), 0)
        nc.gpsimd.memset(w3s_raw[:].bitcast(I32), 0)
        nc.gpsimd.memset(w4s_raw[:].bitcast(I32), 0)

        warm = keep.tile([P, 2], F32, name="warm")
        nc.gpsimd.memset(warm[:, 0:1], 1.0)
        nc.scalar.activation(warm[:, 1:2], warm[:, 0:1], ACT.Sqrt)

        def load_raw(wi, b, piece):
            c0 = PASS * b + W_PIECE * piece
            rows = (w1, w2)[wi][:, c0 : c0 + W_PIECE]
            nc.sync.dma_start(raw[wi, b, piece][:], rows.rearrange("(p j) c -> p j c", j=PACK))

        def load_scale_rows(tile, rows):
            for r in range(4):
                nc.sync.dma_start(tile[r:P:QUADRANT, :].bitcast(I32), rows[r:16:4, :].bitcast(I32))

        nc.sync.dma_start(offs_sb[:], offs)
        load_raw(0, 0, 0)
        load_scale_rows(tabs, tab_scales[0])
        load_raw(0, 0, 1)
        nc.sync.dma_start(w3w_raw[:].bitcast(I32), w3_words[0].bitcast(I32))
        nc.sync.dma_start(tabw[:], tab_words[0].rearrange("p t i -> p (t i)").bitcast(I32))
        load_scale_rows(w3s_raw, w3_scales[0])
        load_raw(1, 0, 0)
        load_raw(1, 0, 1)
        nc.sync.dma_start(pos1_sb[:], pos1)
        nc.sync.dma_start(pos2_sb[:], pos2)
        nc.sync.dma_start(gh_sb[:], gh.rearrange("(b p t) -> p b t", b=2, t=PACK))
        for wi in range(2):
            for piece in range(2):
                load_raw(wi, 1, piece)
        for a in range(2):
            nc.sync.dma_start(w4w_raw[a][:], w4_words[a].rearrange("p c i -> p (c i)").bitcast(I32))
        for q in range(4):
            nc.sync.dma_start(
                w4s_raw[QUADRANT * q : QUADRANT * q + 8, :].bitcast(I32), w4_scales[:, 4 * q : 4 * q + 4, :].bitcast(I32)
            )
        nc.sync.dma_start(pos3_sb[:], pos3)

        vw = keep.tile([P, S], U32, name="vw", align_bytes=64)
        vs = keep.tile([P, S], U8, name="vs", align_bytes=64)
        nc.vector.tensor_copy(vs[:], tabs[:].indirect(offs_sb[:]))

        wq = {}
        ws = {}

        def weave_w(copy, wi, b, piece):
            m0 = W_PIECE // PACK * piece
            dst = woven_w[wi][:, :, m0 : m0 + W_PIECE // PACK, :].rearrange("p t m j -> p m j t")
            copy(dst, raw[wi, b, piece][:].rearrange("p j (m t) -> p m j t", t=PACK))

        def quantise_w(wi, b, t0, t1):
            if t0 == 0:
                wq[wi, b] = keep.tile([P, PASS], U32, name="wq%d%d" % (wi, b), align_bytes=64)
                ws[wi, b] = keep.tile([P, PASS], U8, name="ws%d%d" % (wi, b), align_bytes=64)
            nc.vector.quantize_mx(
                out=wq[wi, b][:, P * t0 : P * t1].bitcast(FP8X4),
                scales=ws[wi, b][:, P * t0 : P * t1],
                in_=woven_w[wi][:, t0:t1].rearrange("p t m j -> p (t m j)"),
            )

        w3w = [keep.tile([P, 2 * PASS], U8, name="w3w%d" % b, align_bytes=64) for b in range(2)]
        w3s = [keep.tile([P, PASS], U8, name="w3s%d" % b, align_bytes=64) for b in range(2)]

        def deal_w3(b):
            nc.vector.tensor_copy(
                w3w[b][:].bitcast(U16).rearrange("p (t m) -> p m t", t=PACK),
                w3w_raw[:, 2 * PASS * b : 2 * PASS * (b + 1)].bitcast(U16).rearrange("p (m t) -> p m t", t=PACK),
            )
            nc.gpsimd.tensor_copy(
                w3s[b][:].rearrange("p (t m) -> p t m", t=PACK),
                w3s_raw[:, PASS * b : PASS * (b + 1)].rearrange("p (m t) -> p t m", t=PACK),
            )

        weave_w(nc.scalar.copy, 0, 0, 0)
        weave_w(nc.scalar.copy, 0, 0, 1)
        deal_w3(0)
        deal_w3(1)
        quantise_w(0, 0, 0, PACK)
        for j0 in range(0, S, BANK):
            nc.vector.tensor_copy(
                vw[:, j0 : j0 + BANK], tabw[:].bitcast(U32).indirect(entries(offs_sb, j0, j0 + BANK))
            )
        weave_w(nc.scalar.copy, 1, 0, 0)
        weave_w(nc.vector.tensor_copy, 1, 0, 1)
        quantise_w(1, 0, 0, 1)

        w4w = [keep.tile([P, H], U32, name="w4w%d" % a, align_bytes=64) for a in range(2)]
        w4s = keep.tile([P, H], U8, name="w4s", align_bytes=64)

        def deal_w4_words(a):
            for b in range(2):
                nc.scalar.copy(
                    w4w[a][:, PASS * b : PASS * (b + 1)].rearrange("p (t m) -> p m t", t=PACK),
                    w4w_raw[a][:, PASS * b : PASS * (b + 1)].bitcast(U32).rearrange("p (m t) -> p m t", t=PACK),
                )

        def deal_w4_scales():
            nc.gpsimd.tensor_copy(
                w4s[:].rearrange("p (b t m) -> p b t m", b=2, t=PACK),
                w4s_raw[:].rearrange("p (b m t) -> p b t m", b=2, t=PACK),
            )

        z = [keep.tile([P, PACK, NOTES], F32, name="z%d" % b) for b in range(2)]
        acc = [keep.tile([P, S], F32, name="acc%d" % i)[:] for i in range(LAST)]
        acc.append(z[1][:, 0:2, :].rearrange("p t m -> p (t m)"))
        gh_last = gh_sb[:, 1, PACK - 1 : PACK]
        gh_last_squared = keep.tile([P, 1], F32, name="gh_last_squared")
        nc.gpsimd.tensor_tensor(gh_last_squared[:], gh_last, gh_last, ALU.mult)
        woven_z = [keep.tile([P, NOTES, PACK], BF16, name="woven_z%d" % b, align_bytes=64) for b in range(2)]
        zq = [keep.tile([P, NOTES], U32, name="zq%d" % b, align_bytes=64) for b in range(2)]
        zs = [keep.tile([P, NOTES], U8, name="zs%d" % b, align_bytes=64) for b in range(2)]

        def z_rows(i):
            return z[i // PACK][:, i % PACK, :]

        def half(ap, jh):
            return ap[:, BANK * jh : BANK * (jh + 1)]

        def stain_of(i):
            return flat(raw[1, 0, 0]) if i == 0 else stain_ring[i % len(stain_ring)][:]

        def clean_of(i, jh):
            if i in DIFF_ON_VECTOR:
                return clean_bank[jh][:]
            return clean_ring[i % len(clean_ring)][:] if jh == 0 else z_rows(i - 1)

        def worse_of(i, jh):
            return worse_ring[(2 * i + jh) % len(worse_ring)][:]

        def h_of(i):
            return h_ring[i % len(h_ring)][:]

        def product(into, words, scales, jh):
            nc.tensor.matmul_mx(
                out=into[:], lhsT=words, lhsT_scale=scales,
                rhs=half(vw, jh).bitcast(FP8X4), rhs_scale=half(vs, jh), start=True, stop=True,
            )

        def products(i):
            b, t = divmod(i, PACK)
            c = slice(P * t, P * (t + 1))
            for jh in range(2):
                product(stain_bank[jh], wq[0, b][:, c].bitcast(FP8X4), ws[0, b][:, c], jh)
                nc.scalar.copy(half(stain_of(i), jh), stain_bank[jh][:])
            for jh in range(2):
                product(crease_bank[jh], wq[1, b][:, c].bitcast(FP8X4), ws[1, b][:, c], jh)
                product(clean_bank[jh], w3w[b][:, 2 * P * t : 2 * P * (t + 1)].bitcast(FP4X4), w3s[b][:, c], jh)
                if i not in DIFF_ON_VECTOR:
                    nc.scalar.copy(clean_of(i, jh), clean_bank[jh][:])

        def take_max(i, jh):
            nc.vector.tensor_tensor(worse_of(i, jh), crease_bank[jh][:], half(stain_of(i), jh), ALU.max)

        def take_diff(i, jh):
            engine = nc.vector if i in DIFF_ON_VECTOR else nc.gpsimd
            engine.tensor_tensor(half(h_of(i), jh), worse_of(i, jh), clean_of(i, jh), ALU.subtract)

        def pair_up(i):
            front, back = half(stain_of(i + 1), 0), half(stain_of(i + 1), 1)
            nc.vector.tensor_copy(front, h_of(i).indirect(pos1_sb[:]))
            nc.vector.tensor_copy(back, h_of(i).indirect(pos2_sb[:]))
            nc.gpsimd.tensor_tensor(z_rows(i), back, front, ALU.add)

        def square_h(i):
            b, t = divmod(i, PACK)
            nc.scalar.activation(acc[i], h_of(i), ACT.Square, scale=gh_sb[:, b, t : t + 1])

        def weave_z(copy, b, m0, m1):
            dst = woven_z[b][:, m0:m1, :].rearrange("p (c i) t -> p c t i", i=4)
            copy(dst, z[b][:, :, m0:m1].rearrange("p t (c i) -> p c t i", i=4))

        def quantise_z(b):
            nc.vector.quantize_mx(
                out=zq[b][:].bitcast(FP8X4), scales=zs[b][:], in_=woven_z[b][:].rearrange("p m t -> p (m t)")
            )

        mid = NOTES // 2
        products(0)
        for i in range(TILES):
            take_max(i, 0)
            if i == 0:
                quantise_w(1, 0, 1, PACK)
            take_max(i, 1)
            take_diff(i, 0)
            take_diff(i, 1)
            if i == QUANTISE_STEP:
                quantise_w(0, 1, 0, PACK)
                quantise_w(1, 1, 0, PACK)
            if i < LAST:
                products(i + 1)
            if i > 0:
                pair_up(i - 1)
            if i < 2:
                weave_w(nc.scalar.copy, i, 1, 0)
            if i == QUANTISE_STEP - 1:
                weave_w(nc.scalar.copy, 0, 1, 1)
                weave_w(nc.scalar.copy, 1, 1, 1)
            if i == QUANTISE_STEP:
                deal_w4_scales()
                for done in range(i):
                    square_h(done)
            if i == QUANTISE_STEP + 1:
                square_h(i - 1)
            if i >= LAST - 1:
                deal_w4_words(i - (LAST - 1))
            if i in (LAST - 2, LAST - 1):
                m0 = mid * (i - (LAST - 2))
                weave_z(nc.scalar.copy, 0, m0, m0 + mid)
        quantise_z(0)
        for i in range(QUANTISE_STEP + 1, LAST - 1):
            square_h(i)

        front = clean_ring[LAST % len(clean_ring)]
        for m0 in (0, mid):
            nc.vector.tensor_copy(front[:, m0 : m0 + mid], h_of(LAST).indirect(entries(pos1_sb, m0, m0 + mid)))
        for m0, copy in ((0, nc.scalar.copy), (mid, nc.vector.tensor_copy)):
            picked = h_of(LAST).indirect(entries(pos2_sb, m0, m0 + mid))
            nc.vector.tensor_tensor(z_rows(LAST)[:, m0 : m0 + mid], picked, front[:, m0 : m0 + mid], ALU.add)
            weave_z(copy, 1, m0, m0 + mid)
        quantise_z(1)
        square_h(LAST - 1)
        nc.vector.scalar_tensor_tensor(acc[LAST], h_of(LAST), gh_last_squared[:], h_of(LAST), ALU.mult, ALU.mult)

        y = [keep.tile([P, NOTES + SPARE], F32, name="y%d" % i) for i in range(TILES)]
        for i in range(TILES):
            nc.gpsimd.memset(y[i][:, NOTES : NOTES + SPARE], 0.0)
        for i in range(TILES):
            c = slice(P * i, P * (i + 1))
            for a in range(2):
                nc.tensor.matmul_mx(
                    out=bank[i][:], lhsT=w4w[a][:, c].bitcast(FP8X4), lhsT_scale=w4s[4 * a : P, c],
                    rhs=zq[a][:].bitcast(FP8X4), rhs_scale=zs[a][:], start=(a == 0), stop=(a == 1),
                )

        def fetch_y(i):
            nc.scalar.copy(y[i][:, 0:NOTES], bank[i][:])

        up_ring = [flat(raw[0, 0, 0]), flat(raw[0, 0, 1]), flat(raw[1, 0, 1])]
        out_rows = out.rearrange("(b p t) j -> b t p j", b=2, t=PACK)

        def pick_square_add(i, j0, j1):
            up = up_ring[i % len(up_ring)]
            for g0 in range(j0, j1, BANK):
                g1 = min(g0 + BANK, j1)
                nc.vector.tensor_copy(up[:, g0:g1], y[i][:].indirect(entries(pos3_sb, g0, g1)))
            nc.scalar.activation(up[:, j0:j1], up[:, j0:j1], ACT.Square)
            engine = nc.vector if i == LAST else nc.gpsimd
            engine.tensor_tensor(acc[i][:, j0:j1], acc[i][:, j0:j1], up[:, j0:j1], ALU.add)

        def root_and_store(i, j0, j1):
            b, t = divmod(i, PACK)
            nc.scalar.activation(acc[i][:, j0:j1], acc[i][:, j0:j1], ACT.Sqrt)
            nc.sync.dma_start(out_rows[b, t][:, j0:j1], acc[i][:, j0:j1])

        for i in range(Y_AHEAD):
            fetch_y(i)
        fetch_behind = [range(3, 4), range(4, 7), range(7, 8)]
        pending = []
        for i in range(TILES):
            width = S // PIECES[i]
            for j0 in range(0, S, width):
                pick_square_add(i, j0, j0 + width)
                if fetch_behind:
                    for later in fetch_behind.pop(0):
                        fetch_y(later)
                pending.append((i, j0, j0 + width))
                while S * (i - pending[0][0]) + j0 + width - pending[0][2] >= S:
                    root_and_store(*pending.pop(0))
        for piece in pending:
            root_and_store(*piece)
